import numpy as np
import ml_dtypes

BF16 = ml_dtypes.bfloat16


def bf(x):
    return np.asarray(x, np.float32).astype(BF16)


def f32(x):
    return np.asarray(x, np.float32)


def f64(x):
    return np.asarray(x).astype(np.float64)


def striped(idx):
    return np.tile(idx.reshape(-1, 16).T, (8, 1))


def rows(idx, k):
    return np.tile(idx, (k, 1))


def look(tab, idx):
    return np.take_along_axis(f64(tab), rows(idx, len(tab)), axis=1)


K, S, V, N = 256, 2048, 1536, 1536


def setup_inputs():
    return {"tab": f32(np.random.standard_normal((2, K, S))), "offs": striped(np.random.permutation(S)[:N])}


def reference(tab, offs):
    idx = offs[:16].T.reshape(-1)
    x = (np.minimum(np.maximum(look(tab[0], idx), -1.25), 1.0)) * (np.maximum(look(tab[1], idx), 0.0))
    return x

@@ -1,0 +1,45 @@
+import concourse.mybir as mybir
+
+F32, U16 = mybir.dt.float32, mybir.dt.uint16
+ALU = mybir.AluOpType
+RELU = mybir.ActivationFunctionType.Relu
+
+LANES = 128
+PIECE = 512
+COLS = PIECE // 16
+
+
+def tile_lookup_vg_cliprelu_out_kernel(tc, tab, offs, out):
+    nc = tc.nc
+    tables, n_rows, places = tab.shape
+    n = out.shape[1]
+    blocks, pieces = n_rows // LANES, n // PIECE
+
+    with (
+        tc.tile_pool(name="held", bufs=1) as held,
+        tc.tile_pool(name="work", bufs=blocks * pieces) as work,
+    ):
+        offsets = held.tile([LANES, n // 16], U16, name="offsets")
+        nc.sync.dma_start(offsets[:], offs)
+
+        values, gates = [], []
+        for b in range(blocks):
+            for table, windows, what in ((0, values, "values"), (1, gates, "gates")):
+                window = held.tile([LANES, places], F32, name=f"{what}{b}")
+                nc.sync.dma_start(window[:], tab[table, b * LANES : (b + 1) * LANES, :])
+                windows.append(window)
+
+        for b in range(blocks):
+            for q in range(pieces):
+                idx = offsets[:, q * COLS : (q + 1) * COLS]
+                clamped = work.tile([LANES, PIECE], F32, name="clamped")
+                nc.vector.tensor_scalar(
+                    clamped[:], values[b][:].indirect(idx), -1.25, 1.0, op0=ALU.max, op1=ALU.min
+                )
+                gate = work.tile([LANES, PIECE], F32, name="gate")
+                nc.scalar.activation(gate[:], gates[b][:].indirect(idx), RELU)
+                product = work.tile([LANES, PIECE], F32, name="product")
+                nc.vector.tensor_tensor(product[:], clamped[:], gate[:], ALU.mult)
+                nc.sync.dma_start(
+                    out[b * LANES : (b + 1) * LANES, q * PIECE : (q + 1) * PIECE], product[:]
+                )

@@ -5,7 +5,7 @@ ALU = mybir.AluOpType
 RELU = mybir.ActivationFunctionType.Relu
 
 LANES = 128
-PIECE = 512
+PIECE = 256
 COLS = PIECE // 16
 
 
@@ -19,6 +19,11 @@ def tile_lookup_vg_cliprelu_out_kernel(tc, tab, offs, out):
         tc.tile_pool(name="held", bufs=1) as held,
         tc.tile_pool(name="work", bufs=blocks * pieces) as work,
     ):
+        zero = held.tile([LANES, 1], F32, name="zero")
+        warm = held.tile([LANES, 1], F32, name="warm")
+        nc.vector.memset(zero[:], 0.0)
+        nc.scalar.activation(warm[:], zero[:], RELU)
+
         offsets = held.tile([LANES, n // 16], U16, name="offsets")
         nc.sync.dma_start(offsets[:], offs)
 
@@ -30,16 +35,22 @@ def tile_lookup_vg_cliprelu_out_kernel(tc, tab, offs, out):
                 windows.append(window)
 
         for b in range(blocks):
+            rows = slice(b * LANES, (b + 1) * LANES)
+
+            clamped = []
             for q in range(pieces):
                 idx = offsets[:, q * COLS : (q + 1) * COLS]
-                clamped = work.tile([LANES, PIECE], F32, name="clamped")
+                value = work.tile([LANES, PIECE], F32, name="value")
                 nc.vector.tensor_scalar(
-                    clamped[:], values[b][:].indirect(idx), -1.25, 1.0, op0=ALU.max, op1=ALU.min
+                    value[:], values[b][:].indirect(idx), -1.25, 1.0, op0=ALU.max, op1=ALU.min
                 )
+                clamped.append(value)
+
+            multiplier = nc.vector if b == blocks - 1 else nc.gpsimd
+            for q in range(pieces):
+                idx = offsets[:, q * COLS : (q + 1) * COLS]
                 gate = work.tile([LANES, PIECE], F32, name="gate")
                 nc.scalar.activation(gate[:], gates[b][:].indirect(idx), RELU)
                 product = work.tile([LANES, PIECE], F32, name="product")
-                nc.vector.tensor_tensor(product[:], clamped[:], gate[:], ALU.mult)
-                nc.sync.dma_start(
-                    out[b * LANES : (b + 1) * LANES, q * PIECE : (q + 1) * PIECE], product[:]
-                )
+                multiplier.tensor_tensor(product[:], clamped[q][:], gate[:], ALU.mult)
+                nc.sync.dma_start(out[rows, q * PIECE : (q + 1) * PIECE], product[:])

@@ -5,19 +5,22 @@ ALU = mybir.AluOpType
 RELU = mybir.ActivationFunctionType.Relu
 
 LANES = 128
-PIECE = 256
-COLS = PIECE // 16
+STEP = 256
+PIECES = [3 * STEP, 2 * STEP, STEP]
 
 
 def tile_lookup_vg_cliprelu_out_kernel(tc, tab, offs, out):
     nc = tc.nc
     tables, n_rows, places = tab.shape
     n = out.shape[1]
-    blocks, pieces = n_rows // LANES, n // PIECE
+    blocks = n_rows // LANES
+    assert sum(PIECES) == n
+    ends = [sum(PIECES[: q + 1]) for q in range(len(PIECES))]
+    spans = [(end - size, end) for size, end in zip(PIECES, ends)]
 
     with (
         tc.tile_pool(name="held", bufs=1) as held,
-        tc.tile_pool(name="work", bufs=blocks * pieces) as work,
+        tc.tile_pool(name="work", bufs=blocks * len(PIECES)) as work,
     ):
         zero = held.tile([LANES, 1], F32, name="zero")
         warm = held.tile([LANES, 1], F32, name="warm")
@@ -38,19 +41,19 @@ def tile_lookup_vg_cliprelu_out_kernel(tc, tab, offs, out):
             rows = slice(b * LANES, (b + 1) * LANES)
 
             clamped = []
-            for q in range(pieces):
-                idx = offsets[:, q * COLS : (q + 1) * COLS]
-                value = work.tile([LANES, PIECE], F32, name="value")
+            for first, end in spans:
+                idx = offsets[:, first // 16 : end // 16]
+                value = work.tile([LANES, end - first], F32, name="value")
                 nc.vector.tensor_scalar(
                     value[:], values[b][:].indirect(idx), -1.25, 1.0, op0=ALU.max, op1=ALU.min
                 )
                 clamped.append(value)
 
             multiplier = nc.vector if b == blocks - 1 else nc.gpsimd
-            for q in range(pieces):
-                idx = offsets[:, q * COLS : (q + 1) * COLS]
-                gate = work.tile([LANES, PIECE], F32, name="gate")
+            for (first, end), value in zip(spans, clamped):
+                idx = offsets[:, first // 16 : end // 16]
+                gate = work.tile([LANES, end - first], F32, name="gate")
                 nc.scalar.activation(gate[:], gates[b][:].indirect(idx), RELU)
-                product = work.tile([LANES, PIECE], F32, name="product")
-                multiplier.tensor_tensor(product[:], clamped[q][:], gate[:], ALU.mult)
-                nc.sync.dma_start(out[rows, q * PIECE : (q + 1) * PIECE], product[:])
+                product = work.tile([LANES, end - first], F32, name="product")
+                multiplier.tensor_tensor(product[:], value[:], gate[:], ALU.mult)
+                nc.sync.dma_start(out[rows, first:end], product[:])

import concourse.mybir as mybir

F32, U16 = mybir.dt.float32, mybir.dt.uint16
ALU = mybir.AluOpType
RELU = mybir.ActivationFunctionType.Relu

LANES = 128
STEP = 256
PIECES = [3 * STEP, 2 * STEP, STEP]


def tile_lookup_vg_cliprelu_out_kernel(tc, tab, offs, out):
    nc = tc.nc
    tables, n_rows, places = tab.shape
    n = out.shape[1]
    blocks = n_rows // LANES
    assert sum(PIECES) == n
    ends = [sum(PIECES[: q + 1]) for q in range(len(PIECES))]
    spans = [(end - size, end) for size, end in zip(PIECES, ends)]

    with (
        tc.tile_pool(name="held", bufs=1) as held,
        tc.tile_pool(name="work", bufs=blocks * len(PIECES)) as work,
    ):
        zero = held.tile([LANES, 1], F32, name="zero")
        warm = held.tile([LANES, 1], F32, name="warm")
        nc.vector.memset(zero[:], 0.0)
        nc.scalar.activation(warm[:], zero[:], RELU)

        offsets = held.tile([LANES, n // 16], U16, name="offsets")
        nc.sync.dma_start(offsets[:], offs)

        values, gates = [], []
        for b in range(blocks):
            for table, windows, what in ((0, values, "values"), (1, gates, "gates")):
                window = held.tile([LANES, places], F32, name=f"{what}{b}")
                nc.sync.dma_start(window[:], tab[table, b * LANES : (b + 1) * LANES, :])
                windows.append(window)

        for b in range(blocks):
            rows = slice(b * LANES, (b + 1) * LANES)

            clamped = []
            for first, end in spans:
                idx = offsets[:, first // 16 : end // 16]
                value = work.tile([LANES, end - first], F32, name="value")
                nc.vector.tensor_scalar(
                    value[:], values[b][:].indirect(idx), -1.25, 1.0, op0=ALU.max, op1=ALU.min
                )
                clamped.append(value)

            multiplier = nc.vector if b == blocks - 1 else nc.gpsimd
            for (first, end), value in zip(spans, clamped):
                idx = offsets[:, first // 16 : end // 16]
                gate = work.tile([LANES, end - first], F32, name="gate")
                nc.scalar.activation(gate[:], gates[b][:].indirect(idx), RELU)
                product = work.tile([LANES, end - first], F32, name="product")
                multiplier.tensor_tensor(product[:], value[:], gate[:], ALU.mult)
                nc.sync.dma_start(out[rows, first:end], product[:])
